import numpy as np
CORES = [40,41,42,43,44,45,46,47,80,81,82,83,84,85,86,87]
N = 16
def setup_inputs(rng):
    return {"x": rng.standard_normal((N, 128, 128), dtype=np.float32)}
def reference(x):
    s = np.maximum.accumulate(x, axis=0)
    y = np.full(x.shape, np.nan, x.dtype)
    y[1:] = s[:-1]
    return {"y": y}

@@ -1,0 +1,132 @@
+from concourse.bass import DstId, RemoteDMATransfer
+
+NS = 8
+W = 16
+
+SCRATCH = {
+    "xs": ("dram", [NS, 128, W], "float32"),
+    "gat": ("dram", [2 * NS, 128, W], "float32"),
+    "m": ("dram", [1, 128, W], "float32"),
+    "bb": ("dram", [4, 128, W], "float32"),
+    "land": ("dram", [NS, 128, W], "float32"),
+}
+SEMAPHORES = ["ld", "gath", "bnc", "res", "sent", "st"]
+
+PHASES = ["s1", "cross", "fold", "bounce"]
+
+
+def plan(cores, topo):
+    a, b = cores[:8], cores[8:]
+    recs = []
+
+    def add(src, phase, srcs, dsts, sem, eng):
+        recs.append((src, phase, srcs, dsts, sem, eng))
+
+    workers = [r for r in range(8) if topo.may_write(a[r], b[0])]
+    idle = [r for r in range(2, 8) if r not in workers]
+    per = NS // len(workers)
+
+    for r in range(8):
+        for s in range(NS):
+            w = workers[s // per]
+            dsts = []
+            if w != r:
+                dsts.append((a[w], "gat", per * r + s % per))
+            if r == 0:
+                dsts.append((a[1], "land", s))
+            if dsts:
+                add(a[r], "s1", [("xs", s)], dsts, "gath", 2)
+
+    for s in range(NS):
+        add(a[1], "fold", [("land", s), ("xs", s)], [(a[2], "land", s)], "res", 2)
+
+    used = {r: 0 for r in idle}
+    bounced = []
+    for k, w in enumerate(workers):
+        for s in range(per * k, per * k + per):
+            src = [("xs", s) if i == w else ("gat", per * i + s % per) for i in range(8)]
+            add(a[w], "cross", src, [(b[s], "land", 0) if s == 0 else (b[s], "m", 0)], "gath", 4)
+            for j in range(3, 8):
+                if j != w:
+                    add(a[w], "fold", src[:j], [(a[j], "land", s)], "res", 1)
+                else:
+                    bo = idle[k % len(idle)]
+                    add(a[w], "fold", src[:j], [(a[bo], "bb", used[bo])], "bnc", 1)
+                    bounced.append((bo, used[bo], w, s))
+                    used[bo] += 1
+    for bo, slot, w, s in bounced:
+        add(a[bo], "bounce", [("bb", slot)], [(a[w], "land", s)], "res", 16 // used[bo])
+
+    for i in range(7):
+        for s in range(NS):
+            if s != i:
+                add(b[i], "s1", [("xs", s)], [(b[s], "gat", i)], "gath", 2)
+    for s in range(NS):
+        src = [("land", 0) if s == 0 else ("m", 0)] + [("xs", s) if i == s else ("gat", i) for i in range(7)]
+        for j in range(8):
+            if j != s:
+                add(b[s], "fold", src[:j + 1], [(b[j], "land", s)], "res", 2)
+            elif s > 0:
+                add(b[s], "fold", src[:j + 1], [(b[s - 1], "bb", 0)], "bnc", 2)
+                add(b[s - 1], "bounce", [("bb", 0)], [(b[s], "land", s)], "res", 16)
+    return recs
+
+
+def rank_program(g, core, T, topo):
+    rank = T.rank_of(core)
+    if rank is None:
+        return
+    recs = plan(T.cores, topo)
+
+    expect = {"gath": 0, "bnc": 0, "res": 0}
+    for _src, _ph, _srcs, dsts, sem, eng in recs:
+        for d in dsts:
+            if d[0] == core:
+                expect[sem] += eng
+    mine = {ph: [r for r in recs if r[0] == core and r[1] == ph] for ph in PHASES}
+    reads_x = any(bs[0] == "xs" for ph in PHASES for r in mine[ph] for bs in r[2])
+
+    sent = [0]
+
+    def issue(phase):
+        if not mine[phase]:
+            return
+        off_chip = phase == "cross"
+        pos = 0 if off_chip else 16
+        trs = []
+        for _src, _ph, srcs, dsts, sem, eng in mine[phase]:
+            if off_chip:
+                mask = ((1 << eng) - 1) << pos
+                pos += eng
+            else:
+                pos -= eng
+                mask = ((1 << eng) - 1) << pos
+            ids = []
+            for d in dsts:
+                rid, pid, _se = topo.addr(d[0])
+                ids.append(DstId(rid=rid, pnc=pid))
+            trs.append(RemoteDMATransfer(
+                dst_ids=ids, dma_engine_mask=mask, remote_sem=T.sem[sem],
+                srcs=[T[bf][sl] for bf, sl in srcs], dsts=[T[d[1]][d[2]] for d in dsts],
+                alu_op=2 if len(srcs) > 1 else 0))
+            sent[0] += eng
+        g.remote_dma_fused(trs, local_sem=T.sem.sent)
+
+    if reads_x:
+        g.dma_start(T.xs[:], T.x[:]).then_inc(T.sem.ld, 16)
+        g.wait_ge(T.sem.ld, 16)
+    issue("s1")
+    if expect["gath"]:
+        g.wait_ge(T.sem.gath, expect["gath"])
+    issue("cross")
+    issue("fold")
+    if expect["bnc"]:
+        g.wait_ge(T.sem.bnc, expect["bnc"])
+    issue("bounce")
+    if expect["res"]:
+        g.wait_ge(T.sem.res, expect["res"])
+    if rank > 0:
+        g.dma_start(T.y[:], T.land[:]).then_inc(T.sem.st, 16)
+        g.wait_ge(T.sem.st, 16)
+    if sent[0]:
+        g.wait_ge(T.sem.sent, sent[0])

@@ -112,6 +112,12 @@ def rank_program(g, core, T, topo):
             sent[0] += eng
         g.remote_dma_fused(trs, local_sem=T.sem.sent)
 
+    if rank > 0:
+        for sem in ("gath", "res"):
+            if any(d[0] == core and d[1] == "land" for r in recs if r[4] == sem for d in r[3]):
+                g.sync.wait_ge(T.sem[sem], expect[sem])
+        g.sync.dma_start(T.y[:], T.land[:]).then_inc(T.sem.st, 16)
+
     if reads_x:
         g.dma_start(T.xs[:], T.x[:]).then_inc(T.sem.ld, 16)
         g.wait_ge(T.sem.ld, 16)
@@ -126,7 +132,6 @@ def rank_program(g, core, T, topo):
     if expect["res"]:
         g.wait_ge(T.sem.res, expect["res"])
     if rank > 0:
-        g.dma_start(T.y[:], T.land[:]).then_inc(T.sem.st, 16)
         g.wait_ge(T.sem.st, 16)
     if sent[0]:
         g.wait_ge(T.sem.sent, sent[0])

from concourse.bass import DstId, RemoteDMATransfer

NS = 8
W = 16

SCRATCH = {
    "xs": ("dram", [NS, 128, W], "float32"),
    "gat": ("dram", [2 * NS, 128, W], "float32"),
    "m": ("dram", [1, 128, W], "float32"),
    "bb": ("dram", [4, 128, W], "float32"),
    "land": ("dram", [NS, 128, W], "float32"),
}
SEMAPHORES = ["ld", "gath", "bnc", "res", "sent", "st"]

PHASES = ["s1", "cross", "fold", "bounce"]


def plan(cores, topo):
    a, b = cores[:8], cores[8:]
    recs = []

    def add(src, phase, srcs, dsts, sem, eng):
        recs.append((src, phase, srcs, dsts, sem, eng))

    workers = [r for r in range(8) if topo.may_write(a[r], b[0])]
    idle = [r for r in range(2, 8) if r not in workers]
    per = NS // len(workers)

    for r in range(8):
        for s in range(NS):
            w = workers[s // per]
            dsts = []
            if w != r:
                dsts.append((a[w], "gat", per * r + s % per))
            if r == 0:
                dsts.append((a[1], "land", s))
            if dsts:
                add(a[r], "s1", [("xs", s)], dsts, "gath", 2)

    for s in range(NS):
        add(a[1], "fold", [("land", s), ("xs", s)], [(a[2], "land", s)], "res", 2)

    used = {r: 0 for r in idle}
    bounced = []
    for k, w in enumerate(workers):
        for s in range(per * k, per * k + per):
            src = [("xs", s) if i == w else ("gat", per * i + s % per) for i in range(8)]
            add(a[w], "cross", src, [(b[s], "land", 0) if s == 0 else (b[s], "m", 0)], "gath", 4)
            for j in range(3, 8):
                if j != w:
                    add(a[w], "fold", src[:j], [(a[j], "land", s)], "res", 1)
                else:
                    bo = idle[k % len(idle)]
                    add(a[w], "fold", src[:j], [(a[bo], "bb", used[bo])], "bnc", 1)
                    bounced.append((bo, used[bo], w, s))
                    used[bo] += 1
    for bo, slot, w, s in bounced:
        add(a[bo], "bounce", [("bb", slot)], [(a[w], "land", s)], "res", 16 // used[bo])

    for i in range(7):
        for s in range(NS):
            if s != i:
                add(b[i], "s1", [("xs", s)], [(b[s], "gat", i)], "gath", 2)
    for s in range(NS):
        src = [("land", 0) if s == 0 else ("m", 0)] + [("xs", s) if i == s else ("gat", i) for i in range(7)]
        for j in range(8):
            if j != s:
                add(b[s], "fold", src[:j + 1], [(b[j], "land", s)], "res", 2)
            elif s > 0:
                add(b[s], "fold", src[:j + 1], [(b[s - 1], "bb", 0)], "bnc", 2)
                add(b[s - 1], "bounce", [("bb", 0)], [(b[s], "land", s)], "res", 16)
    return recs


def rank_program(g, core, T, topo):
    rank = T.rank_of(core)
    if rank is None:
        return
    recs = plan(T.cores, topo)

    expect = {"gath": 0, "bnc": 0, "res": 0}
    for _src, _ph, _srcs, dsts, sem, eng in recs:
        for d in dsts:
            if d[0] == core:
                expect[sem] += eng
    mine = {ph: [r for r in recs if r[0] == core and r[1] == ph] for ph in PHASES}
    reads_x = any(bs[0] == "xs" for ph in PHASES for r in mine[ph] for bs in r[2])

    sent = [0]

    def issue(phase):
        if not mine[phase]:
            return
        off_chip = phase == "cross"
        pos = 0 if off_chip else 16
        trs = []
        for _src, _ph, srcs, dsts, sem, eng in mine[phase]:
            if off_chip:
                mask = ((1 << eng) - 1) << pos
                pos += eng
            else:
                pos -= eng
                mask = ((1 << eng) - 1) << pos
            ids = []
            for d in dsts:
                rid, pid, _se = topo.addr(d[0])
                ids.append(DstId(rid=rid, pnc=pid))
            trs.append(RemoteDMATransfer(
                dst_ids=ids, dma_engine_mask=mask, remote_sem=T.sem[sem],
                srcs=[T[bf][sl] for bf, sl in srcs], dsts=[T[d[1]][d[2]] for d in dsts],
                alu_op=2 if len(srcs) > 1 else 0))
            sent[0] += eng
        g.remote_dma_fused(trs, local_sem=T.sem.sent)

    if rank > 0:
        for sem in ("gath", "res"):
            if any(d[0] == core and d[1] == "land" for r in recs if r[4] == sem for d in r[3]):
                g.sync.wait_ge(T.sem[sem], expect[sem])
        g.sync.dma_start(T.y[:], T.land[:]).then_inc(T.sem.st, 16)

    if reads_x:
        g.dma_start(T.xs[:], T.x[:]).then_inc(T.sem.ld, 16)
        g.wait_ge(T.sem.ld, 16)
    issue("s1")
    if expect["gath"]:
        g.wait_ge(T.sem.gath, expect["gath"])
    issue("cross")
    issue("fold")
    if expect["bnc"]:
        g.wait_ge(T.sem.bnc, expect["bnc"])
    issue("bounce")
    if expect["res"]:
        g.wait_ge(T.sem.res, expect["res"])
    if rank > 0:
        g.wait_ge(T.sem.st, 16)
    if sent[0]:
        g.wait_ge(T.sem.sent, sent[0])
